import numpy as np
import ml_dtypes


def mxq(x, axis, fmt="e4m3"):
    dtype, down = {"e4m3": (ml_dtypes.float8_e4m3fn, 7), "e5m2": (ml_dtypes.float8_e5m2, 14)}[fmt]
    v = np.moveaxis(np.asarray(x, np.float32).astype(ml_dtypes.bfloat16).astype(np.float64), axis, -1)
    blocks = v.reshape(v.shape[:-1] + (-1, 32))
    amax = np.abs(blocks).max(-1, keepdims=True)
    byte = np.maximum(np.where(amax > 0, np.frexp(amax)[1] - 1 + 127, 0) - down, 1)
    scale = np.exp2(byte - 127.0)
    codes = (blocks / scale).astype(np.float32).astype(dtype).astype(np.float64)
    return np.moveaxis((codes * scale).reshape(v.shape), -1, axis)


WIDE = False


def mx_kscale(k):
    if not WIDE:
        return np.ones(k)
    levels = np.array([10, -10, 5, -5, 0])
    if k % 512:
        return np.exp2(np.random.permutation(np.resize(levels, k // 32))).repeat(32)
    a = np.empty((k // 512, 16))
    for p in range(k // 512):
        a[p, :8] = np.random.permutation(np.resize(levels, 8))
        for g in range(8):
            far = levels[np.abs(levels - a[p, g]) >= 10]
            a[p, g + 8] = far[np.random.randint(len(far))]
    return np.exp2(a.ravel()).repeat(32)


def f64(x):
    return np.asarray(x).astype(np.float64)


def striped(idx):
    return np.tile(idx.reshape(-1, 16).T, (8, 1)).astype(np.uint16)


def unstriped(offs):
    return offs[:16].T.reshape(-1).astype(np.int64)


def gelu(v):
    return 0.5 * v * (1.0 + np.tanh(np.sqrt(2.0 / np.pi) * (v + 0.044715 * v**3)))


K, T, E, C, H, N = 1024, 640, 8, 128, 512, 128
TOP = 4
PAD = 64


def by_expert(wq, xq):
    return np.concatenate([wq[e].T @ xq[:, e * C:(e + 1) * C] for e in range(E)], axis=1)


def setup_inputs():
    n = np.random.standard_normal
    s = mx_kscale(K)[:, None]
    u = mx_kscale(H)
    slot_token = np.empty(E * C, np.int64); pos = np.tile(E * C + np.arange(T) % PAD, (TOP, 1)); taken = np.zeros(T, np.int64)
    liked = np.random.randn(T)
    for e in np.random.permutation(E):
        free = np.flatnonzero(taken < TOP); pick = np.random.permutation(free[np.argsort(-(liked[free] + np.random.gumbel(size=free.size)))[:C]]); slot_token[e * C:(e + 1) * C] = pick
        pos[taken[pick], pick] = e * C + np.arange(C); taken[pick] += 1
    g = np.random.uniform(0.2, 0.8, (TOP, T))
    return {
        "xT": (n((K, T)) * s).astype(np.float32),
        "w1": (n((E, K, H)) / np.sqrt(K) / s[None]).astype(np.float32),
        "w3": (n((E, K, H)) / np.sqrt(K) / s[None] * u[None, None, :]).astype(np.float32),
        "w2": (n((E, H, N)) / np.sqrt(H) / u[None, :, None]).astype(np.float32),
        "gate": np.stack([np.tile(r, (N, 1)) for r in g]).astype(np.float32),
        "offs": striped(slot_token),
        "pos1": striped(pos[0]),
        "pos2": striped(pos[1]),
        "pos3": striped(pos[2]),
        "pos4": striped(pos[3]),
    }


def reference(xT, w1, w3, w2, gate, offs, pos1, pos2, pos3, pos4):
    idx = unstriped(offs)
    xq = mxq(f64(xT)[:, idx], 0, "e4m3")
    h = gelu(by_expert(mxq(f64(w1), 1, "e4m3"), xq))
    h = h * by_expert(mxq(f64(w3), 1, "e4m3"), xq)
    y = by_expert(mxq(f64(w2), 1, "e4m3"), mxq(h, 0, "e4m3"))
    y = np.concatenate([y, np.zeros((N, PAD))], axis=1)
    return sum(f64(gate[r]) * y[:, unstriped(p)] for r, p in enumerate((pos1, pos2, pos3, pos4)))

@@ -1,0 +1,226 @@
+from contextlib import ExitStack
+
+import concourse.mybir as mybir
+from concourse.masks import make_identity
+
+K, T, E, C, H, N = 1024, 640, 8, 128, 512, 128
+TOP = 4
+PAD = 64
+
+F32 = mybir.dt.float32
+BF16 = mybir.dt.bfloat16
+U32 = mybir.dt.uint32
+U16 = mybir.dt.uint16
+U8 = mybir.dt.uint8
+FP8X4 = mybir.dt.float8_e4m3fn_x4
+MULT = mybir.AluOpType.mult
+ADD = mybir.AluOpType.add
+COPY = mybir.ActivationFunctionType.Copy
+GELU = mybir.ActivationFunctionType.Gelu_apprx_tanh
+
+P = 128
+PACK = 4
+K_PASS = P * PACK
+PASSES = K // K_PASS
+LIST_ROWS = 16
+RUN = 4
+RING = 12
+SCALAR_COLS = 288
+X_SCALAR_COLS = 256
+W2_GROUP = 2
+TOKEN_CUTS = (0, 256, 512, 640)
+
+FLOPS = 2 * E * C * (2 * K * H + H * N)
+
+
+def interleave_views(grouped, raw):
+    dst = grouped.rearrange("p (c i) j -> p c j i", i=RUN)
+    src = raw.rearrange("p j (c i) -> p c j i", i=RUN)
+    return dst, src
+
+
+def tile_moe_ecr_glu_gelu_kernel(
+    tc, xT, w1, w3, w2, gate, offs, pos1, pos2, pos3, pos4, out
+):
+    nc = tc.nc
+    with ExitStack() as ctx:
+        keep = ctx.enter_context(tc.tile_pool(name="keep", bufs=1))
+        ring = ctx.enter_context(tc.tile_pool(name="ring", bufs=RING))
+        stage = ctx.enter_context(tc.tile_pool(name="stage", bufs=4))
+        small = ctx.enter_context(tc.tile_pool(name="small", bufs=2))
+        psum = ctx.enter_context(tc.psum_pool(name="psum", bufs=2))
+
+        x_raw = []
+        for a in range(PASSES):
+            raw = keep.tile([P, PACK, T], F32, name="x_raw%d" % a)
+            nc.sync.dma_start(out=raw[:], in_=xT[a * K_PASS : (a + 1) * K_PASS, :].rearrange("(p j) t -> p j t", j=PACK))
+            x_raw.append(raw)
+        slot_list = keep.tile([P, E * C // LIST_ROWS], U16, name="slot_list")
+        nc.sync.dma_start(slot_list[:], offs)
+
+        ident = keep.tile([P, P], F32, name="ident")
+        make_identity(nc, ident[:])
+        x_scales = keep.tile([P, T], U8, name="x_scales", align_bytes=64)
+        nc.gpsimd.memset(x_scales[:], 0)
+        y_all = keep.tile([P, E * C + PAD], F32, name="y_all")
+        nc.gpsimd.memset(y_all[:, E * C :], 0.0)
+
+        x_words = []
+        for a in range(PASSES):
+            grouped = keep.tile([P, T, PACK], BF16, name="x_grouped%d" % a, align_bytes=64)
+            dst, src = interleave_views(grouped[:, :X_SCALAR_COLS, :], x_raw[a][:, :, :X_SCALAR_COLS])
+            nc.scalar.activation(out=dst, in_=src, func=COPY)
+            dst, src = interleave_views(grouped[:, X_SCALAR_COLS:, :], x_raw[a][:, :, X_SCALAR_COLS:])
+            nc.vector.tensor_copy(out=dst, in_=src)
+            words = keep.tile([P, T], U32, name="x_words%d" % a, align_bytes=64)
+            for t0, t1 in ((0, 512), (512, T)):
+                nc.vector.quantize_mx(
+                    out=words[:, t0:t1].bitcast(FP8X4),
+                    scales=x_scales[PACK * a :, t0:t1],
+                    in_=grouped[:, t0:t1, :].rearrange("p t j -> p (t j)"),
+                )
+            x_words.append(words)
+
+        def gather_tokens(e):
+            entries = slot_list[:, e * C // LIST_ROWS : (e + 1) * C // LIST_ROWS]
+            slot_scales = small.tile([P, C], U8, name="slot_scales", align_bytes=64)
+            nc.vector.tensor_copy(out=slot_scales[:], in_=x_scales[:].indirect(entries))
+            slot_words = []
+            for a in range(PASSES):
+                words = small.tile([P, C], U32, name="slot_words%d" % a, align_bytes=64)
+                nc.vector.tensor_copy(out=words[:], in_=x_words[a][:].indirect(entries))
+                slot_words.append(words)
+            return slot_words, slot_scales
+
+        def first_layer_pass(w, e, a, acc, slot_words, slot_scales):
+            raw = ring.tile([P, PACK, H], F32, name="w_raw", tag="ring")
+            nc.sync.dma_start(out=raw[:], in_=w[e, a * K_PASS : (a + 1) * K_PASS, :].rearrange("(p j) h -> p j h", j=PACK))
+            grouped = stage.tile([P, H, PACK], BF16, name="w_grouped", align_bytes=64)
+            dst, src = interleave_views(grouped[:, :SCALAR_COLS, :], raw[:, :, :SCALAR_COLS])
+            nc.scalar.copy(out=dst, in_=src)
+            dst, src = interleave_views(grouped[:, SCALAR_COLS:, :], raw[:, :, SCALAR_COLS:])
+            nc.vector.tensor_copy(out=dst, in_=src)
+            words = stage.tile([P, H], U32, name="w_words", align_bytes=64)
+            scales = stage.tile([P, H], U8, name="w_scales", align_bytes=64)
+            nc.vector.quantize_mx(
+                out=words[:].bitcast(FP8X4), scales=scales[:], in_=grouped[:].rearrange("p h j -> p (h j)")
+            )
+            nc.tensor.matmul_mx(
+                out=acc[:],
+                lhsT=slot_words[a][:].bitcast(FP8X4),
+                lhsT_scale=slot_scales[PACK * a :, :],
+                rhs=words[:].bitcast(FP8X4),
+                rhs_scale=scales[:],
+                start=(a == 0),
+                stop=(a == PASSES - 1),
+            )
+
+        def hidden(e):
+            slot_words, slot_scales = gather_tokens(e)
+            acc1 = psum.tile([C, H], F32, name="acc1")
+            acc3 = psum.tile([C, H], F32, name="acc3")
+            for a in range(PASSES):
+                first_layer_pass(w1, e, a, acc1, slot_words, slot_scales)
+                first_layer_pass(w3, e, a, acc3, slot_words, slot_scales)
+            act = small.tile([C, 2, P, 2], F32, name="act")
+            nc.scalar.activation(out=act[:], in_=acc1[:].rearrange("c (p u v) -> c u p v", u=2, v=2), func=GELU)
+            h_rows = small.tile([C, H], BF16, name="h_rows")
+            nc.vector.tensor_tensor(
+                out=h_rows[:].rearrange("c (u p v) -> c u p v", u=2, v=2),
+                in0=acc3[:].rearrange("c (p u v) -> c u p v", u=2, v=2),
+                in1=act[:],
+                op=MULT,
+            )
+            pairs = h_rows[:].bitcast(F32)
+            turned = psum.tile([P, 2, C], F32, name="turned")
+            for u in range(2):
+                nc.tensor.transpose(turned[:, u, :], pairs[:, u * P : (u + 1) * P], ident[:])
+            h_grouped = small.tile([P, C * PACK], BF16, name="h_grouped", align_bytes=64)
+            nc.scalar.copy(
+                out=h_grouped[:].bitcast(F32).rearrange("p (c u) -> p c u", u=2),
+                in_=turned[:].rearrange("p u c -> p c u"),
+            )
+            words = keep.tile([P, C], U32, name="h_words%d" % e, align_bytes=64)
+            scales = keep.tile([P, C], U8, name="h_scales%d" % e, align_bytes=64)
+            nc.vector.quantize_mx(out=words[:].bitcast(FP8X4), scales=scales[:], in_=h_grouped[:])
+            return words, scales
+
+        def second_layer(e0, h_codes):
+            raw = ring.tile([P, W2_GROUP, PACK, N], F32, name="w2_raw", tag="ring")
+            nc.sync.dma_start(
+                out=raw[:].rearrange("p e j n -> p e (j n)"),
+                in_=w2[e0 : e0 + W2_GROUP].rearrange("e (p j) n -> p e (j n)", j=PACK),
+            )
+            grouped = small.tile([P, W2_GROUP, N, PACK], BF16, name="w2_grouped", align_bytes=64)
+            for d, copy in enumerate((nc.scalar.copy, nc.vector.tensor_copy)):
+                dst, src = interleave_views(grouped[:, d], raw[:, d])
+                copy(out=dst, in_=src)
+            words = small.tile([P, W2_GROUP * N], U32, name="w2_words", align_bytes=64)
+            scales = small.tile([P, W2_GROUP * N], U8, name="w2_scales", align_bytes=64)
+            nc.vector.quantize_mx(
+                out=words[:].bitcast(FP8X4), scales=scales[:], in_=grouped[:].rearrange("p e n j -> p (e n j)")
+            )
+            for d in range(W2_GROUP):
+                e = e0 + d
+                h_words, h_scales = h_codes[e]
+                y = psum.tile([N, C], F32, name="y")
+                nc.tensor.matmul_mx(
+                    out=y[:],
+                    lhsT=words[:, d * N : (d + 1) * N].bitcast(FP8X4),
+                    lhsT_scale=scales[:, d * N : (d + 1) * N],
+                    rhs=h_words[:].bitcast(FP8X4),
+                    rhs_scale=h_scales[:],
+                    start=True,
+                    stop=True,
+                )
+                nc.scalar.copy(out=y_all[:, e * C : (e + 1) * C], in_=y[:])
+
+        h_codes = [hidden(e) for e in range(E)]
+        for e0 in range(0, E, W2_GROUP):
+            second_layer(e0, h_codes)
+
+        places = []
+        for r, pos in enumerate((pos1, pos2, pos3, pos4)):
+            place = keep.tile([P, T // LIST_ROWS], U16, name="place%d" % r)
+            nc.sync.dma_start(place[:], pos)
+            places.append(place)
+        for t0, t1 in zip(TOKEN_CUTS, TOKEN_CUTS[1:]):
+            width = t1 - t0
+            gates = ring.tile([P, TOP, width], F32, name="gates", tag="ring")
+            nc.sync.dma_start(out=gates[:], in_=gate[:, :, t0:t1].rearrange("r n t -> n r t"))
+            terms = []
+            for r in range(TOP):
+                term = keep.tile([P, width], F32, name="term%d_%d" % (t0, r))
+                nc.vector.tensor_tensor(
+                    out=term[:],
+                    in0=y_all[:].indirect(places[r][:, t0 // LIST_ROWS : t1 // LIST_ROWS]),
+                    in1=gates[:, r, :],
+                    op=MULT,
+                )
+                terms.append(term)
+            total = keep.tile([P, width], F32, name="total%d" % t0)
+            if t1 < T:
+                summed = psum.tile([P, width], F32, name="summed", tag="acc1")
+                for b0 in range(0, width, P):
+                    for r in range(TOP):
+                        nc.tensor.matmul(
+                            summed[:, b0 : b0 + P],
+                            lhsT=terms[r][:, b0 : b0 + P],
+                            rhs=ident[:],
+                            is_transpose=True,
+                            start=(r == 0),
+                            stop=(r == TOP - 1),
+                        )
+                by_token = small.tile([P, width], F32, name="by_token")
+                nc.scalar.copy(out=by_token[:], in_=summed[:])
+                back = psum.tile([P, width], F32, name="back", tag="acc3")
+                for b0 in range(0, width, P):
+                    nc.tensor.transpose(back[:, b0 : b0 + P], by_token[:, b0 : b0 + P], ident[:])
+                nc.scalar.copy(out=total[:], in_=back[:])
+            else:
+                two = small.tile([P, width], F32, name="two")
+                nc.vector.tensor_tensor(out=two[:], in0=terms[0][:], in1=terms[1][:], op=ADD)
+                three = small.tile([P, width], F32, name="three")
+                nc.vector.tensor_tensor(out=three[:], in0=two[:], in1=terms[2][:], op=ADD)
+                nc.vector.tensor_tensor(out=total[:], in0=three[:], in1=terms[3][:], op=ADD)
+            nc.sync.dma_start(out=out[:, t0:t1], in_=total[:])

@@ -24,10 +24,13 @@ K_PASS = P * PACK
 PASSES = K // K_PASS
 LIST_ROWS = 16
 RUN = 4
-RING = 12
-SCALAR_COLS = 288
+RING = 7
+SCALAR_SHARE = 9
+GATHER = 256
+WHOLE_LOADS = 6
+LAST_SCALAR_SHARE = 6
 X_SCALAR_COLS = 256
-W2_GROUP = 2
+W2_CUTS = (0, 4, 6, 8)
 TOKEN_CUTS = (0, 256, 512, 640)
 
 FLOPS = 2 * E * C * (2 * K * H + H * N)
@@ -46,13 +49,13 @@ def tile_moe_ecr_glu_gelu_kernel(
     with ExitStack() as ctx:
         keep = ctx.enter_context(tc.tile_pool(name="keep", bufs=1))
         ring = ctx.enter_context(tc.tile_pool(name="ring", bufs=RING))
-        stage = ctx.enter_context(tc.tile_pool(name="stage", bufs=4))
+        stage = ctx.enter_context(tc.tile_pool(name="stage", bufs=3))
         small = ctx.enter_context(tc.tile_pool(name="small", bufs=2))
         psum = ctx.enter_context(tc.psum_pool(name="psum", bufs=2))
 
         x_raw = []
         for a in range(PASSES):
-            raw = keep.tile([P, PACK, T], F32, name="x_raw%d" % a)
+            raw = ring.tile([P, PACK, T], F32, name="x_raw", tag="ring", align_bytes=64)
             nc.sync.dma_start(out=raw[:], in_=xT[a * K_PASS : (a + 1) * K_PASS, :].rearrange("(p j) t -> p j t", j=PACK))
             x_raw.append(raw)
         slot_list = keep.tile([P, E * C // LIST_ROWS], U16, name="slot_list")
@@ -81,103 +84,163 @@ def tile_moe_ecr_glu_gelu_kernel(
                 )
             x_words.append(words)
 
-        def gather_tokens(e):
-            entries = slot_list[:, e * C // LIST_ROWS : (e + 1) * C // LIST_ROWS]
-            slot_scales = small.tile([P, C], U8, name="slot_scales", align_bytes=64)
-            nc.vector.tensor_copy(out=slot_scales[:], in_=x_scales[:].indirect(entries))
-            slot_words = []
+        slot_scales = keep.tile([P, E * C], U8, name="slot_scales", align_bytes=64)
+        slot_words = [keep.tile([P, E * C], U32, name="slot_words%d" % a, align_bytes=64) for a in range(PASSES)]
+        for s0 in range(0, E * C, GATHER):
+            slots = slice(s0, s0 + GATHER)
+            entries = slot_list[:, s0 // LIST_ROWS : (s0 + GATHER) // LIST_ROWS]
+            nc.vector.tensor_copy(out=slot_scales[:, slots], in_=x_scales[:].indirect(entries))
             for a in range(PASSES):
-                words = small.tile([P, C], U32, name="slot_words%d" % a, align_bytes=64)
-                nc.vector.tensor_copy(out=words[:], in_=x_words[a][:].indirect(entries))
-                slot_words.append(words)
-            return slot_words, slot_scales
+                nc.vector.tensor_copy(out=slot_words[a][:, slots], in_=x_words[a][:].indirect(entries))
 
-        def first_layer_pass(w, e, a, acc, slot_words, slot_scales):
-            raw = ring.tile([P, PACK, H], F32, name="w_raw", tag="ring")
-            nc.sync.dma_start(out=raw[:], in_=w[e, a * K_PASS : (a + 1) * K_PASS, :].rearrange("(p j) h -> p j h", j=PACK))
-            grouped = stage.tile([P, H, PACK], BF16, name="w_grouped", align_bytes=64)
-            dst, src = interleave_views(grouped[:, :SCALAR_COLS, :], raw[:, :, :SCALAR_COLS])
-            nc.scalar.copy(out=dst, in_=src)
-            dst, src = interleave_views(grouped[:, SCALAR_COLS:, :], raw[:, :, SCALAR_COLS:])
-            nc.vector.tensor_copy(out=dst, in_=src)
-            words = stage.tile([P, H], U32, name="w_words", align_bytes=64)
-            scales = stage.tile([P, H], U8, name="w_scales", align_bytes=64)
+        def weight_codes(w, e, a0, a1, h0, h1, share):
+            passes, width = a1 - a0, h1 - h0
+            raw = ring.tile([P, passes, PACK, width], F32, name="w_raw", tag="ring", align_bytes=64)
+            rows = w[e, a0 * K_PASS : a1 * K_PASS, h0:h1]
+            if passes == 1:
+                nc.sync.dma_start(out=raw[:, 0], in_=rows.rearrange("(p j) h -> p j h", j=PACK))
+            else:
+                nc.sync.dma_start(
+                    out=raw[:].rearrange("p a j h -> p a (j h)"),
+                    in_=rows.rearrange("(a p j) h -> p a (j h)", p=P, j=PACK),
+                )
+            grouped = stage.tile([P, passes, width, PACK], BF16, name="w_grouped", align_bytes=64)
+            cut = passes * width * share // 16
+            for a in range(passes):
+                own = min(max(cut - a * width, 0), width)
+                for copy, c0, c1 in ((nc.scalar.copy, 0, own), (nc.vector.tensor_copy, own, width)):
+                    if c1 > c0:
+                        dst, src = interleave_views(grouped[:, a, c0:c1, :], raw[:, a, :, c0:c1])
+                        copy(out=dst, in_=src)
+            words = stage.tile([P, passes, width], U32, name="w_words", align_bytes=64)
+            scales = stage.tile([P, passes, width], U8, name="w_scales", align_bytes=64)
             nc.vector.quantize_mx(
-                out=words[:].bitcast(FP8X4), scales=scales[:], in_=grouped[:].rearrange("p h j -> p (h j)")
+                out=words[:].rearrange("p a h -> p (a h)").bitcast(FP8X4),
+                scales=scales[:].rearrange("p a h -> p (a h)"),
+                in_=grouped[:].rearrange("p a h j -> p (a h j)"),
             )
+            return [(words[:, a, :], scales[:, a, :]) for a in range(passes)], raw[:].rearrange("p a j h -> p (a j h)")
+
+        def multiply(acc, e, a, codes, cols):
+            slots = slice(e * C, (e + 1) * C)
+            words, scales = codes
             nc.tensor.matmul_mx(
-                out=acc[:],
-                lhsT=slot_words[a][:].bitcast(FP8X4),
-                lhsT_scale=slot_scales[PACK * a :, :],
-                rhs=words[:].bitcast(FP8X4),
-                rhs_scale=scales[:],
+                out=acc,
+                lhsT=slot_words[a][:, slots].bitcast(FP8X4),
+                lhsT_scale=slot_scales[PACK * a :, slots],
+                rhs=words[:, cols].bitcast(FP8X4),
+                rhs_scale=scales[:, cols],
                 start=(a == 0),
                 stop=(a == PASSES - 1),
             )
 
-        def hidden(e):
-            slot_words, slot_scales = gather_tokens(e)
-            acc1 = psum.tile([C, H], F32, name="acc1")
-            acc3 = psum.tile([C, H], F32, name="acc3")
-            for a in range(PASSES):
-                first_layer_pass(w1, e, a, acc1, slot_words, slot_scales)
-                first_layer_pass(w3, e, a, acc3, slot_words, slot_scales)
-            act = small.tile([C, 2, P, 2], F32, name="act")
-            nc.scalar.activation(out=act[:], in_=acc1[:].rearrange("c (p u v) -> c u p v", u=2, v=2), func=GELU)
-            h_rows = small.tile([C, H], BF16, name="h_rows")
-            nc.vector.tensor_tensor(
-                out=h_rows[:].rearrange("c (u p v) -> c u p v", u=2, v=2),
-                in0=acc3[:].rearrange("c (p u v) -> c u p v", u=2, v=2),
-                in1=act[:],
-                op=MULT,
-            )
-            pairs = h_rows[:].bitcast(F32)
-            turned = psum.tile([P, 2, C], F32, name="turned")
+        def pair_order(ap):
+            return ap.rearrange("c (p u v) -> c u p v", u=2, v=2)
+
+        def pair_view(ap):
+            return ap.rearrange("c (u p v) -> c u p v", u=2, v=2)
+
+        def hidden_codes(e, h_rows, h_grouped):
+            pairs = h_rows.bitcast(F32)
+            turned = psum.tile([P, 2, C], F32, name="turned", bufs=1)
             for u in range(2):
                 nc.tensor.transpose(turned[:, u, :], pairs[:, u * P : (u + 1) * P], ident[:])
-            h_grouped = small.tile([P, C * PACK], BF16, name="h_grouped", align_bytes=64)
             nc.scalar.copy(
-                out=h_grouped[:].bitcast(F32).rearrange("p (c u) -> p c u", u=2),
+                out=h_grouped.bitcast(F32).rearrange("p (c u) -> p c u", u=2),
                 in_=turned[:].rearrange("p u c -> p c u"),
             )
             words = keep.tile([P, C], U32, name="h_words%d" % e, align_bytes=64)
             scales = keep.tile([P, C], U8, name="h_scales%d" % e, align_bytes=64)
-            nc.vector.quantize_mx(out=words[:].bitcast(FP8X4), scales=scales[:], in_=h_grouped[:])
+            nc.vector.quantize_mx(out=words[:].bitcast(FP8X4), scales=scales[:], in_=h_grouped)
             return words, scales
 
-        def second_layer(e0, h_codes):
-            raw = ring.tile([P, W2_GROUP, PACK, N], F32, name="w2_raw", tag="ring")
+        def w2_codes(e0, e1, on_scalar):
+            count = e1 - e0
+            raw = ring.tile([P, count, PACK, N], F32, name="w2_raw", tag="ring", align_bytes=64)
             nc.sync.dma_start(
                 out=raw[:].rearrange("p e j n -> p e (j n)"),
-                in_=w2[e0 : e0 + W2_GROUP].rearrange("e (p j) n -> p e (j n)", j=PACK),
+                in_=w2[e0:e1].rearrange("e (p j) n -> p e (j n)", j=PACK),
             )
-            grouped = small.tile([P, W2_GROUP, N, PACK], BF16, name="w2_grouped", align_bytes=64)
-            for d, copy in enumerate((nc.scalar.copy, nc.vector.tensor_copy)):
-                dst, src = interleave_views(grouped[:, d], raw[:, d])
-                copy(out=dst, in_=src)
-            words = small.tile([P, W2_GROUP * N], U32, name="w2_words", align_bytes=64)
-            scales = small.tile([P, W2_GROUP * N], U8, name="w2_scales", align_bytes=64)
+            grouped = small.tile([P, count, N, PACK], BF16, name="w2_grouped", align_bytes=64)
+            for copy, d0, d1 in ((nc.scalar.copy, 0, on_scalar), (nc.vector.tensor_copy, on_scalar, count)):
+                if d1 > d0:
+                    copy(
+                        out=grouped[:, d0:d1].rearrange("p e (c i) j -> p e c j i", i=RUN),
+                        in_=raw[:, d0:d1].rearrange("p e j (c i) -> p e c j i", i=RUN),
+                    )
+            words = small.tile([P, count * N], U32, name="w2_words", align_bytes=64)
+            scales = small.tile([P, count * N], U8, name="w2_scales", align_bytes=64)
             nc.vector.quantize_mx(
                 out=words[:].bitcast(FP8X4), scales=scales[:], in_=grouped[:].rearrange("p e n j -> p (e n j)")
             )
-            for d in range(W2_GROUP):
-                e = e0 + d
-                h_words, h_scales = h_codes[e]
-                y = psum.tile([N, C], F32, name="y")
-                nc.tensor.matmul_mx(
-                    out=y[:],
-                    lhsT=words[:, d * N : (d + 1) * N].bitcast(FP8X4),
-                    lhsT_scale=scales[:, d * N : (d + 1) * N],
-                    rhs=h_words[:].bitcast(FP8X4),
-                    rhs_scale=h_scales[:],
-                    start=True,
-                    stop=True,
-                )
-                nc.scalar.copy(out=y_all[:, e * C : (e + 1) * C], in_=y[:])
+            codes = [(words[:, d * N : (d + 1) * N], scales[:, d * N : (d + 1) * N]) for d in range(count)]
+            return codes, raw[:].rearrange("p e j n -> p (e j n)")
 
-        h_codes = [hidden(e) for e in range(E)]
-        for e0 in range(0, E, W2_GROUP):
-            second_layer(e0, h_codes)
+        def slot_results(e, weights, hidden):
+            y = psum.tile([N, C], F32, name="y")
+            nc.tensor.matmul_mx(
+                out=y[:],
+                lhsT=weights[0].bitcast(FP8X4),
+                lhsT_scale=weights[1],
+                rhs=hidden[0][:].bitcast(FP8X4),
+                rhs_scale=hidden[1][:],
+                start=True,
+                stop=True,
+            )
+            nc.scalar.copy(out=y_all[:, e * C : (e + 1) * C], in_=y[:])
+
+        every = slice(0, H)
+        half = H // 2
+        h_codes = []
+        act = acc3 = None
+        for e in range(E):
+            step = PASSES if e < WHOLE_LOADS else 1
+            acc1 = psum.tile([C, H], F32, name="acc1")
+            loads = [(w, a0) for w in (w1, w3) for a0 in range(0, PASSES, step)]
+            if e == E - 1:
+                loads = loads[:-1]
+            for i, (w, a0) in enumerate(loads):
+                codes, raw = weight_codes(w, e, a0, a0 + step, 0, H, SCALAR_SHARE)
+                if w is w1:
+                    for a, pass_codes in enumerate(codes, a0):
+                        multiply(acc1[:], e, a, pass_codes, every)
+                if e > 0 and i == 0:
+                    size = step * PACK * H
+                    h_rows = raw[:, size - half : size].bitcast(BF16)
+                    nc.vector.tensor_tensor(out=pair_view(h_rows), in0=pair_order(acc3[:]), in1=act, op=MULT)
+                if e > 0 and i == 1:
+                    h_codes.append(hidden_codes(e - 1, h_rows, raw[:, H : H + half].bitcast(BF16)))
+                if w is w3 and a0 == 0:
+                    act = pair_view(raw[:, 0:H])
+                    nc.scalar.activation(out=act, in_=pair_order(acc1[:]), func=GELU)
+                    if e < E - 1:
+                        acc3 = psum.tile([C, H], F32, name="acc3")
+                if w is w3 and e < E - 1:
+                    for a, pass_codes in enumerate(codes, a0):
+                        multiply(acc3[:], e, a, pass_codes, every)
+            if e == W2_CUTS[1]:
+                early_weights, raw = w2_codes(W2_CUTS[0], W2_CUTS[1], W2_CUTS[1] // 2)
+                for d, weights in enumerate(early_weights):
+                    slot_results(d, weights, h_codes[d])
+        accs = [psum.tile([C, half], F32, name="acc3") for s in range(2)]
+        for s in range(2):
+            multiply(accs[s][:], E - 1, 0, codes[0], slice(s * half, (s + 1) * half))
+        for s in range(2):
+            codes, raw = weight_codes(w3, E - 1, 1, 2, s * half, (s + 1) * half, LAST_SCALAR_SHARE)
+            multiply(accs[s][:], E - 1, 1, codes[0], slice(0, half))
+        h_rows = raw[:, PACK * half - half :].bitcast(BF16)
+        for s in range(2):
+            part = slice(s * P // 2, (s + 1) * P // 2)
+            nc.vector.tensor_tensor(
+                out=pair_view(h_rows)[:, :, part, :], in0=pair_order(accs[s][:]), in1=act[:, :, part, :], op=MULT
+            )
+        late_weights = []
+        for e0, e1 in zip(W2_CUTS[1:], W2_CUTS[2:]):
+            codes, raw = w2_codes(e0, e1, e1 - e0)
+            late_weights.extend(codes)
+        h_codes.append(hidden_codes(E - 1, h_rows, raw[:, 0:half].bitcast(BF16)))
+        for e, weights in enumerate(late_weights, W2_CUTS[1]):
+            slot_results(e, weights, h_codes[e])
 
         places = []
         for r, pos in enumerate((pos1, pos2, pos3, pos4)):
@@ -186,7 +249,7 @@ def tile_moe_ecr_glu_gelu_kernel(
             places.append(place)
         for t0, t1 in zip(TOKEN_CUTS, TOKEN_CUTS[1:]):
             width = t1 - t0
-            gates = ring.tile([P, TOP, width], F32, name="gates", tag="ring")
+            gates = ring.tile([P, TOP, width], F32, name="gates", tag="ring", align_bytes=64)
             nc.sync.dma_start(out=gates[:], in_=gate[:, :, t0:t1].rearrange("r n t -> n r t"))
             terms = []
             for r in range(TOP):
@@ -200,11 +263,12 @@ def tile_moe_ecr_glu_gelu_kernel(
                 terms.append(term)
             total = keep.tile([P, width], F32, name="total%d" % t0)
             if t1 < T:
-                summed = psum.tile([P, width], F32, name="summed", tag="acc1")
-                for b0 in range(0, width, P):
-                    for r in range(TOP):
+                blocks = range(0, width, P)
+                sums = [psum.tile([P, P], F32, name="summed", tag="acc1") for b0 in blocks]
+                for r in range(TOP):
+                    for summed, b0 in zip(sums, blocks):
                         nc.tensor.matmul(
-                            summed[:, b0 : b0 + P],
+                            summed[:],
                             lhsT=terms[r][:, b0 : b0 + P],
                             rhs=ident[:],
                             is_transpose=True,
@@ -212,15 +276,17 @@ def tile_moe_ecr_glu_gelu_kernel(
                             stop=(r == TOP - 1),
                         )
                 by_token = small.tile([P, width], F32, name="by_token")
-                nc.scalar.copy(out=by_token[:], in_=summed[:])
+                for summed, b0 in zip(sums, blocks):
+                    nc.scalar.copy(out=by_token[:, b0 : b0 + P], in_=summed[:])
                 back = psum.tile([P, width], F32, name="back", tag="acc3")
                 for b0 in range(0, width, P):
                     nc.tensor.transpose(back[:, b0 : b0 + P], by_token[:, b0 : b0 + P], ident[:])
                 nc.scalar.copy(out=total[:], in_=back[:])
             else:
-                two = small.tile([P, width], F32, name="two")
-                nc.vector.tensor_tensor(out=two[:], in0=terms[0][:], in1=terms[1][:], op=ADD)
-                three = small.tile([P, width], F32, name="three")
-                nc.vector.tensor_tensor(out=three[:], in0=two[:], in1=terms[2][:], op=ADD)
-                nc.vector.tensor_tensor(out=total[:], in0=three[:], in1=terms[3][:], op=ADD)
-            nc.sync.dma_start(out=out[:, t0:t1], in_=total[:])
+                low = small.tile([P, width], F32, name="low")
+                nc.vector.tensor_tensor(out=low[:], in0=terms[0][:], in1=terms[1][:], op=ADD)
+                high = small.tile([P, width], F32, name="high")
+                nc.vector.tensor_tensor(out=high[:], in0=terms[2][:], in1=terms[3][:], op=ADD)
+                nc.vector.tensor_tensor(out=total[:], in0=low[:], in1=high[:], op=ADD)
+            queue = nc.scalar if t1 < T else nc.sync
+            queue.dma_start(out=out[:, t0:t1], in_=total[:])

@@ -30,7 +30,7 @@ GATHER = 256
 WHOLE_LOADS = 6
 LAST_SCALAR_SHARE = 6
 X_SCALAR_COLS = 256
-W2_CUTS = (0, 4, 6, 8)
+W2_CUTS = (0, 2, 4, 6, 8)
 TOKEN_CUTS = (0, 256, 512, 640)
 
 FLOPS = 2 * E * C * (2 * K * H + H * N)
@@ -161,33 +161,35 @@ def tile_moe_ecr_glu_gelu_kernel(
                 out=raw[:].rearrange("p e j n -> p e (j n)"),
                 in_=w2[e0:e1].rearrange("e (p j) n -> p e (j n)", j=PACK),
             )
-            grouped = small.tile([P, count, N, PACK], BF16, name="w2_grouped", align_bytes=64)
+            grouped = small.tile([P, count, N, PACK], BF16, name="w2_grouped", align_bytes=64, bufs=3)
             for copy, d0, d1 in ((nc.scalar.copy, 0, on_scalar), (nc.vector.tensor_copy, on_scalar, count)):
                 if d1 > d0:
                     copy(
                         out=grouped[:, d0:d1].rearrange("p e (c i) j -> p e c j i", i=RUN),
                         in_=raw[:, d0:d1].rearrange("p e j (c i) -> p e c j i", i=RUN),
                     )
-            words = small.tile([P, count * N], U32, name="w2_words", align_bytes=64)
-            scales = small.tile([P, count * N], U8, name="w2_scales", align_bytes=64)
+            words = small.tile([P, count * N], U32, name="w2_words", align_bytes=64, bufs=3)
+            scales = small.tile([P, count * N], U8, name="w2_scales", align_bytes=64, bufs=3)
             nc.vector.quantize_mx(
                 out=words[:].bitcast(FP8X4), scales=scales[:], in_=grouped[:].rearrange("p e n j -> p (e n j)")
             )
             codes = [(words[:, d * N : (d + 1) * N], scales[:, d * N : (d + 1) * N]) for d in range(count)]
             return codes, raw[:].rearrange("p e j n -> p (e j n)")
 
-        def slot_results(e, weights, hidden):
-            y = psum.tile([N, C], F32, name="y")
-            nc.tensor.matmul_mx(
-                out=y[:],
-                lhsT=weights[0].bitcast(FP8X4),
-                lhsT_scale=weights[1],
-                rhs=hidden[0][:].bitcast(FP8X4),
-                rhs_scale=hidden[1][:],
-                start=True,
-                stop=True,
-            )
-            nc.scalar.copy(out=y_all[:, e * C : (e + 1) * C], in_=y[:])
+        def slot_results(e0, weights, bank, copy):
+            y = psum.tile([N, len(weights) * C], F32, name="y", tag=bank, bufs=1)
+            for d, (words, scales) in enumerate(weights):
+                h_words, h_scales = h_codes[e0 + d]
+                nc.tensor.matmul_mx(
+                    out=y[:, d * C : (d + 1) * C],
+                    lhsT=words.bitcast(FP8X4),
+                    lhsT_scale=scales,
+                    rhs=h_words[:].bitcast(FP8X4),
+                    rhs_scale=h_scales[:],
+                    start=True,
+                    stop=True,
+                )
+            copy(out=y_all[:, e0 * C : (e0 + len(weights)) * C], in_=y[:])
 
         every = slice(0, H)
         half = H // 2
@@ -220,8 +222,7 @@ def tile_moe_ecr_glu_gelu_kernel(
                         multiply(acc3[:], e, a, pass_codes, every)
             if e == W2_CUTS[1]:
                 early_weights, raw = w2_codes(W2_CUTS[0], W2_CUTS[1], W2_CUTS[1] // 2)
-                for d, weights in enumerate(early_weights):
-                    slot_results(d, weights, h_codes[d])
+                slot_results(0, early_weights, "y", nc.scalar.copy)
         accs = [psum.tile([C, half], F32, name="acc3") for s in range(2)]
         for s in range(2):
             multiply(accs[s][:], E - 1, 0, codes[0], slice(s * half, (s + 1) * half))
@@ -236,11 +237,12 @@ def tile_moe_ecr_glu_gelu_kernel(
             )
         late_weights = []
         for e0, e1 in zip(W2_CUTS[1:], W2_CUTS[2:]):
-            codes, raw = w2_codes(e0, e1, e1 - e0)
+            codes, raw = w2_codes(e0, e1, e1 - e0 if e1 < E else 1)
             late_weights.extend(codes)
-        h_codes.append(hidden_codes(E - 1, h_rows, raw[:, 0:half].bitcast(BF16)))
-        for e, weights in enumerate(late_weights, W2_CUTS[1]):
-            slot_results(e, weights, h_codes[e])
+            if e1 == W2_CUTS[-2]:
+                h_codes.append(hidden_codes(E - 1, h_rows, raw[:, 0:half].bitcast(BF16)))
+        slot_results(W2_CUTS[1], late_weights[:-2], "turned", nc.scalar.copy)
+        slot_results(W2_CUTS[-2], late_weights[-2:], "y", nc.vector.tensor_copy)
 
         places = []
         for r, pos in enumerate((pos1, pos2, pos3, pos4)):

from contextlib import ExitStack

import concourse.mybir as mybir
from concourse.masks import make_identity

K, T, E, C, H, N = 1024, 640, 8, 128, 512, 128
TOP = 4
PAD = 64

F32 = mybir.dt.float32
BF16 = mybir.dt.bfloat16
U32 = mybir.dt.uint32
U16 = mybir.dt.uint16
U8 = mybir.dt.uint8
FP8X4 = mybir.dt.float8_e4m3fn_x4
MULT = mybir.AluOpType.mult
ADD = mybir.AluOpType.add
COPY = mybir.ActivationFunctionType.Copy
GELU = mybir.ActivationFunctionType.Gelu_apprx_tanh

P = 128
PACK = 4
K_PASS = P * PACK
PASSES = K // K_PASS
LIST_ROWS = 16
RUN = 4
RING = 7
SCALAR_SHARE = 9
GATHER = 256
WHOLE_LOADS = 6
LAST_SCALAR_SHARE = 6
X_SCALAR_COLS = 256
W2_CUTS = (0, 2, 4, 6, 8)
TOKEN_CUTS = (0, 256, 512, 640)

FLOPS = 2 * E * C * (2 * K * H + H * N)


def interleave_views(grouped, raw):
    dst = grouped.rearrange("p (c i) j -> p c j i", i=RUN)
    src = raw.rearrange("p j (c i) -> p c j i", i=RUN)
    return dst, src


def tile_moe_ecr_glu_gelu_kernel(
    tc, xT, w1, w3, w2, gate, offs, pos1, pos2, pos3, pos4, out
):
    nc = tc.nc
    with ExitStack() as ctx:
        keep = ctx.enter_context(tc.tile_pool(name="keep", bufs=1))
        ring = ctx.enter_context(tc.tile_pool(name="ring", bufs=RING))
        stage = ctx.enter_context(tc.tile_pool(name="stage", bufs=3))
        small = ctx.enter_context(tc.tile_pool(name="small", bufs=2))
        psum = ctx.enter_context(tc.psum_pool(name="psum", bufs=2))

        x_raw = []
        for a in range(PASSES):
            raw = ring.tile([P, PACK, T], F32, name="x_raw", tag="ring", align_bytes=64)
            nc.sync.dma_start(out=raw[:], in_=xT[a * K_PASS : (a + 1) * K_PASS, :].rearrange("(p j) t -> p j t", j=PACK))
            x_raw.append(raw)
        slot_list = keep.tile([P, E * C // LIST_ROWS], U16, name="slot_list")
        nc.sync.dma_start(slot_list[:], offs)

        ident = keep.tile([P, P], F32, name="ident")
        make_identity(nc, ident[:])
        x_scales = keep.tile([P, T], U8, name="x_scales", align_bytes=64)
        nc.gpsimd.memset(x_scales[:], 0)
        y_all = keep.tile([P, E * C + PAD], F32, name="y_all")
        nc.gpsimd.memset(y_all[:, E * C :], 0.0)

        x_words = []
        for a in range(PASSES):
            grouped = keep.tile([P, T, PACK], BF16, name="x_grouped%d" % a, align_bytes=64)
            dst, src = interleave_views(grouped[:, :X_SCALAR_COLS, :], x_raw[a][:, :, :X_SCALAR_COLS])
            nc.scalar.activation(out=dst, in_=src, func=COPY)
            dst, src = interleave_views(grouped[:, X_SCALAR_COLS:, :], x_raw[a][:, :, X_SCALAR_COLS:])
            nc.vector.tensor_copy(out=dst, in_=src)
            words = keep.tile([P, T], U32, name="x_words%d" % a, align_bytes=64)
            for t0, t1 in ((0, 512), (512, T)):
                nc.vector.quantize_mx(
                    out=words[:, t0:t1].bitcast(FP8X4),
                    scales=x_scales[PACK * a :, t0:t1],
                    in_=grouped[:, t0:t1, :].rearrange("p t j -> p (t j)"),
                )
            x_words.append(words)

        slot_scales = keep.tile([P, E * C], U8, name="slot_scales", align_bytes=64)
        slot_words = [keep.tile([P, E * C], U32, name="slot_words%d" % a, align_bytes=64) for a in range(PASSES)]
        for s0 in range(0, E * C, GATHER):
            slots = slice(s0, s0 + GATHER)
            entries = slot_list[:, s0 // LIST_ROWS : (s0 + GATHER) // LIST_ROWS]
            nc.vector.tensor_copy(out=slot_scales[:, slots], in_=x_scales[:].indirect(entries))
            for a in range(PASSES):
                nc.vector.tensor_copy(out=slot_words[a][:, slots], in_=x_words[a][:].indirect(entries))

        def weight_codes(w, e, a0, a1, h0, h1, share):
            passes, width = a1 - a0, h1 - h0
            raw = ring.tile([P, passes, PACK, width], F32, name="w_raw", tag="ring", align_bytes=64)
            rows = w[e, a0 * K_PASS : a1 * K_PASS, h0:h1]
            if passes == 1:
                nc.sync.dma_start(out=raw[:, 0], in_=rows.rearrange("(p j) h -> p j h", j=PACK))
            else:
                nc.sync.dma_start(
                    out=raw[:].rearrange("p a j h -> p a (j h)"),
                    in_=rows.rearrange("(a p j) h -> p a (j h)", p=P, j=PACK),
                )
            grouped = stage.tile([P, passes, width, PACK], BF16, name="w_grouped", align_bytes=64)
            cut = passes * width * share // 16
            for a in range(passes):
                own = min(max(cut - a * width, 0), width)
                for copy, c0, c1 in ((nc.scalar.copy, 0, own), (nc.vector.tensor_copy, own, width)):
                    if c1 > c0:
                        dst, src = interleave_views(grouped[:, a, c0:c1, :], raw[:, a, :, c0:c1])
                        copy(out=dst, in_=src)
            words = stage.tile([P, passes, width], U32, name="w_words", align_bytes=64)
            scales = stage.tile([P, passes, width], U8, name="w_scales", align_bytes=64)
            nc.vector.quantize_mx(
                out=words[:].rearrange("p a h -> p (a h)").bitcast(FP8X4),
                scales=scales[:].rearrange("p a h -> p (a h)"),
                in_=grouped[:].rearrange("p a h j -> p (a h j)"),
            )
            return [(words[:, a, :], scales[:, a, :]) for a in range(passes)], raw[:].rearrange("p a j h -> p (a j h)")

        def multiply(acc, e, a, codes, cols):
            slots = slice(e * C, (e + 1) * C)
            words, scales = codes
            nc.tensor.matmul_mx(
                out=acc,
                lhsT=slot_words[a][:, slots].bitcast(FP8X4),
                lhsT_scale=slot_scales[PACK * a :, slots],
                rhs=words[:, cols].bitcast(FP8X4),
                rhs_scale=scales[:, cols],
                start=(a == 0),
                stop=(a == PASSES - 1),
            )

        def pair_order(ap):
            return ap.rearrange("c (p u v) -> c u p v", u=2, v=2)

        def pair_view(ap):
            return ap.rearrange("c (u p v) -> c u p v", u=2, v=2)

        def hidden_codes(e, h_rows, h_grouped):
            pairs = h_rows.bitcast(F32)
            turned = psum.tile([P, 2, C], F32, name="turned", bufs=1)
            for u in range(2):
                nc.tensor.transpose(turned[:, u, :], pairs[:, u * P : (u + 1) * P], ident[:])
            nc.scalar.copy(
                out=h_grouped.bitcast(F32).rearrange("p (c u) -> p c u", u=2),
                in_=turned[:].rearrange("p u c -> p c u"),
            )
            words = keep.tile([P, C], U32, name="h_words%d" % e, align_bytes=64)
            scales = keep.tile([P, C], U8, name="h_scales%d" % e, align_bytes=64)
            nc.vector.quantize_mx(out=words[:].bitcast(FP8X4), scales=scales[:], in_=h_grouped)
            return words, scales

        def w2_codes(e0, e1, on_scalar):
            count = e1 - e0
            raw = ring.tile([P, count, PACK, N], F32, name="w2_raw", tag="ring", align_bytes=64)
            nc.sync.dma_start(
                out=raw[:].rearrange("p e j n -> p e (j n)"),
                in_=w2[e0:e1].rearrange("e (p j) n -> p e (j n)", j=PACK),
            )
            grouped = small.tile([P, count, N, PACK], BF16, name="w2_grouped", align_bytes=64, bufs=3)
            for copy, d0, d1 in ((nc.scalar.copy, 0, on_scalar), (nc.vector.tensor_copy, on_scalar, count)):
                if d1 > d0:
                    copy(
                        out=grouped[:, d0:d1].rearrange("p e (c i) j -> p e c j i", i=RUN),
                        in_=raw[:, d0:d1].rearrange("p e j (c i) -> p e c j i", i=RUN),
                    )
            words = small.tile([P, count * N], U32, name="w2_words", align_bytes=64, bufs=3)
            scales = small.tile([P, count * N], U8, name="w2_scales", align_bytes=64, bufs=3)
            nc.vector.quantize_mx(
                out=words[:].bitcast(FP8X4), scales=scales[:], in_=grouped[:].rearrange("p e n j -> p (e n j)")
            )
            codes = [(words[:, d * N : (d + 1) * N], scales[:, d * N : (d + 1) * N]) for d in range(count)]
            return codes, raw[:].rearrange("p e j n -> p (e j n)")

        def slot_results(e0, weights, bank, copy):
            y = psum.tile([N, len(weights) * C], F32, name="y", tag=bank, bufs=1)
            for d, (words, scales) in enumerate(weights):
                h_words, h_scales = h_codes[e0 + d]
                nc.tensor.matmul_mx(
                    out=y[:, d * C : (d + 1) * C],
                    lhsT=words.bitcast(FP8X4),
                    lhsT_scale=scales,
                    rhs=h_words[:].bitcast(FP8X4),
                    rhs_scale=h_scales[:],
                    start=True,
                    stop=True,
                )
            copy(out=y_all[:, e0 * C : (e0 + len(weights)) * C], in_=y[:])

        every = slice(0, H)
        half = H // 2
        h_codes = []
        act = acc3 = None
        for e in range(E):
            step = PASSES if e < WHOLE_LOADS else 1
            acc1 = psum.tile([C, H], F32, name="acc1")
            loads = [(w, a0) for w in (w1, w3) for a0 in range(0, PASSES, step)]
            if e == E - 1:
                loads = loads[:-1]
            for i, (w, a0) in enumerate(loads):
                codes, raw = weight_codes(w, e, a0, a0 + step, 0, H, SCALAR_SHARE)
                if w is w1:
                    for a, pass_codes in enumerate(codes, a0):
                        multiply(acc1[:], e, a, pass_codes, every)
                if e > 0 and i == 0:
                    size = step * PACK * H
                    h_rows = raw[:, size - half : size].bitcast(BF16)
                    nc.vector.tensor_tensor(out=pair_view(h_rows), in0=pair_order(acc3[:]), in1=act, op=MULT)
                if e > 0 and i == 1:
                    h_codes.append(hidden_codes(e - 1, h_rows, raw[:, H : H + half].bitcast(BF16)))
                if w is w3 and a0 == 0:
                    act = pair_view(raw[:, 0:H])
                    nc.scalar.activation(out=act, in_=pair_order(acc1[:]), func=GELU)
                    if e < E - 1:
                        acc3 = psum.tile([C, H], F32, name="acc3")
                if w is w3 and e < E - 1:
                    for a, pass_codes in enumerate(codes, a0):
                        multiply(acc3[:], e, a, pass_codes, every)
            if e == W2_CUTS[1]:
                early_weights, raw = w2_codes(W2_CUTS[0], W2_CUTS[1], W2_CUTS[1] // 2)
                slot_results(0, early_weights, "y", nc.scalar.copy)
        accs = [psum.tile([C, half], F32, name="acc3") for s in range(2)]
        for s in range(2):
            multiply(accs[s][:], E - 1, 0, codes[0], slice(s * half, (s + 1) * half))
        for s in range(2):
            codes, raw = weight_codes(w3, E - 1, 1, 2, s * half, (s + 1) * half, LAST_SCALAR_SHARE)
            multiply(accs[s][:], E - 1, 1, codes[0], slice(0, half))
        h_rows = raw[:, PACK * half - half :].bitcast(BF16)
        for s in range(2):
            part = slice(s * P // 2, (s + 1) * P // 2)
            nc.vector.tensor_tensor(
                out=pair_view(h_rows)[:, :, part, :], in0=pair_order(accs[s][:]), in1=act[:, :, part, :], op=MULT
            )
        late_weights = []
        for e0, e1 in zip(W2_CUTS[1:], W2_CUTS[2:]):
            codes, raw = w2_codes(e0, e1, e1 - e0 if e1 < E else 1)
            late_weights.extend(codes)
            if e1 == W2_CUTS[-2]:
                h_codes.append(hidden_codes(E - 1, h_rows, raw[:, 0:half].bitcast(BF16)))
        slot_results(W2_CUTS[1], late_weights[:-2], "turned", nc.scalar.copy)
        slot_results(W2_CUTS[-2], late_weights[-2:], "y", nc.vector.tensor_copy)

        places = []
        for r, pos in enumerate((pos1, pos2, pos3, pos4)):
            place = keep.tile([P, T // LIST_ROWS], U16, name="place%d" % r)
            nc.sync.dma_start(place[:], pos)
            places.append(place)
        for t0, t1 in zip(TOKEN_CUTS, TOKEN_CUTS[1:]):
            width = t1 - t0
            gates = ring.tile([P, TOP, width], F32, name="gates", tag="ring", align_bytes=64)
            nc.sync.dma_start(out=gates[:], in_=gate[:, :, t0:t1].rearrange("r n t -> n r t"))
            terms = []
            for r in range(TOP):
                term = keep.tile([P, width], F32, name="term%d_%d" % (t0, r))
                nc.vector.tensor_tensor(
                    out=term[:],
                    in0=y_all[:].indirect(places[r][:, t0 // LIST_ROWS : t1 // LIST_ROWS]),
                    in1=gates[:, r, :],
                    op=MULT,
                )
                terms.append(term)
            total = keep.tile([P, width], F32, name="total%d" % t0)
            if t1 < T:
                blocks = range(0, width, P)
                sums = [psum.tile([P, P], F32, name="summed", tag="acc1") for b0 in blocks]
                for r in range(TOP):
                    for summed, b0 in zip(sums, blocks):
                        nc.tensor.matmul(
                            summed[:],
                            lhsT=terms[r][:, b0 : b0 + P],
                            rhs=ident[:],
                            is_transpose=True,
                            start=(r == 0),
                            stop=(r == TOP - 1),
                        )
                by_token = small.tile([P, width], F32, name="by_token")
                for summed, b0 in zip(sums, blocks):
                    nc.scalar.copy(out=by_token[:, b0 : b0 + P], in_=summed[:])
                back = psum.tile([P, width], F32, name="back", tag="acc3")
                for b0 in range(0, width, P):
                    nc.tensor.transpose(back[:, b0 : b0 + P], by_token[:, b0 : b0 + P], ident[:])
                nc.scalar.copy(out=total[:], in_=back[:])
            else:
                low = small.tile([P, width], F32, name="low")
                nc.vector.tensor_tensor(out=low[:], in0=terms[0][:], in1=terms[1][:], op=ADD)
                high = small.tile([P, width], F32, name="high")
                nc.vector.tensor_tensor(out=high[:], in0=terms[2][:], in1=terms[3][:], op=ADD)
                nc.vector.tensor_tensor(out=total[:], in0=low[:], in1=high[:], op=ADD)
            queue = nc.scalar if t1 < T else nc.sync
            queue.dma_start(out=out[:, t0:t1], in_=total[:])
